import numpy as np
CORES = [13,21,141,149]
N = 4
F = 32
BOUND = 50.6
def setup_inputs(rng):
    gr = rng.standard_normal((1, 128, N * F), dtype=np.float32) + rng.standard_normal((N, 128, N * F), dtype=np.float32)
    gr = gr * (2.0 ** rng.uniform(-3, 3, (1, 128, 1))).astype(np.float32)
    return {"gr": gr}
def setup_inputs_big(rng):
    d = setup_inputs(rng)
    for k in ("gr",): d[k] = (d[k].astype(np.float32) * 1024.0).astype(d[k].dtype)
    return d
def setup_inputs_small(rng):
    d = setup_inputs(rng)
    for k in ("gr",): d[k] = (d[k].astype(np.float32) * (1 / 1024.0)).astype(d[k].dtype)
    return d
def setup_inputs_apart(rng):
    d = setup_inputs(rng)
    f = (10.0 ** rng.permutation(np.linspace(-1.5, 1.5, N))).astype(np.float32).reshape(N, 1, 1)
    for k in ("gr",): d[k] = (d[k].astype(np.float32) * f).astype(d[k].dtype)
    return d
def setup_inputs_mixed(rng):
    d = setup_inputs(rng)
    f = (10.0 ** rng.uniform(-3, 3, (1, 128, 1))).astype(np.float32); shape = rng.integers(2, size=(1, 128, 1))
    for k in ("gr",):
        x = d[k].astype(np.float32)
        other = x * np.where(rng.random((1, 128, N * F)) < 0.5, 0.1, 1.0).astype(np.float32)
        d[k] = (np.where(shape == 1, other, x) * f).astype(d[k].dtype)
    return d
def reference(gr):
    s = gr.astype(np.float64).sum(axis=0)
    nrm = np.sqrt((s ** 2).sum(axis=1, keepdims=True))
    s = s * np.minimum(1.0, BOUND / nrm)
    return {"y": np.stack([s[:, F * r:F * r + F] for r in range(N)]).astype(np.float32)}

@@ -1,0 +1,165 @@
+import math
+from concourse.bass import DstId, RemoteDMATransfer
+from concourse.mybir import AluOpType, AxisListType, ActivationFunctionType
+
+P, WID, BLK = 128, 128, 32
+N1, N2 = 43, 63
+BETA = 2.0 ** -48
+E_STAGE = 4
+E_PEER = 8
+E_CROSS = 8
+
+SCRATCH = {
+    "stage": ("dram", [P, WID], "float32"),
+    "hin": ("dram", [2, P, WID], "float32"),
+    "own": ("sbuf", [P, WID], "float32"),
+    "peer": ("sbuf", [P, WID], "float32"),
+    "cross": ("sbuf", [P, WID], "float32"),
+    "s": ("sbuf", [P, WID], "float32"),
+    "sq": ("sbuf", [P, WID], "float32"),
+    "fill": ("sbuf", [P, 128], "float32"),
+    "th": ("sbuf", [P, 128], "float32"),
+    "fac": ("sbuf", [P, 128], "float32"),
+    "col": ("sbuf", [P, 16], "float32"),
+    "yb": ("sbuf", [P, BLK], "float32"),
+    "p": ("psum", [P, WID], "float32"),
+}
+SEMAPHORES = ["ld_stage", "ld_own", "sent", "hin", "peer_in", "cross_in", "vq", "aq", "st"]
+
+
+def _engines(mask):
+    return [e for e in range(mask.bit_length()) if (mask >> e) & 1]
+
+
+def _spread(lst, n):
+    return lst[::len(lst) // n][:n]
+
+
+def _bits(lst):
+    return sum(1 << e for e in lst)
+
+
+def _plan(T, topo):
+    ranks = list(T.cores)
+    ga = [r for r in ranks if r == ranks[0] or topo.may_write(ranks[0], r)]
+    gb = [r for r in ranks if r not in ga]
+    ncores = (max(topo.host(r) for r in ranks) + 1) * topo.CORES_PER_HOST
+    jobs = []
+    for srcs, dsts in ((ga, gb), (gb, ga)):
+        for i, src in enumerate(srcs):
+            relay = [c for c in range(ncores)
+                     if c not in ranks and topo.host(c) == topo.host(src) and topo.chip(c) == topo.chip(src)
+                     and topo.die(c) == topo.die(src) and topo.may_write(c, dsts[i])][0]
+            jobs.append((relay, srcs, dsts[i]))
+    return ga, gb, jobs
+
+
+def _relay_program(g, core, T, topo, srcs, dst):
+    g.wait_ge(T.sem.hin, E_STAGE * len(srcs))
+    rid, pid = topo.addr(dst, core)
+    m = _bits(_spread(_engines(topo.mask(core, dst)), E_CROSS))
+    g.remote_dma_fused([RemoteDMATransfer(dst_ids=[DstId(rid=rid, pnc=pid)], dma_engine_mask=m, remote_sem=T.sem.cross_in,
+                                          srcs=[T.hin[k] for k in range(len(srcs))], dsts=[T.cross[:, :]], alu_op=1)],
+                       local_sem=T.sem.sent)
+    g.wait_ge(T.sem.sent, E_CROSS)
+
+
+def rank_program(g, core, T, topo):
+    ga, gb, jobs = _plan(T, topo)
+    for relay, srcs, dst in jobs:
+        if relay == core:
+            _relay_program(g, core, T, topo, srcs, dst)
+            return
+    rank = T.rank_of(core)
+    if rank is None:
+        return
+    sem = T.sem
+    group = ga if core in ga else gb
+    partner = [r for r in group if r != core][0]
+    mult, add = AluOpType.mult, AluOpType.add
+
+    g.sync.dma_start(T.stage[:, :], T.gr[:, :]).then_inc(sem.ld_stage, 16)
+    g.sync.dma_start(T.own[:, :], T.gr[:, :]).then_inc(sem.ld_own, 16)
+
+    far = _engines(topo.mask(core, partner))
+    transfers = []
+    for relay, srcs, dst in jobs:
+        if core not in srcs:
+            continue
+        avail = _engines(topo.mask(core, relay))
+        near_only = [e for e in avail if e not in far]
+        eng = _spread(near_only if near_only else avail, E_STAGE)
+        rid, pid = topo.addr(relay, core)
+        transfers.append(RemoteDMATransfer(dst_ids=[DstId(rid=rid, pnc=pid)], dma_engine_mask=_bits(eng), remote_sem=sem.hin,
+                                           src=T.stage[:, :], dst=T.hin[srcs.index(core)]))
+    g.wait_ge(sem.ld_stage, 16)
+    g.remote_dma_fused(transfers, local_sem=sem.sent)
+    rid, pid = topo.addr(partner, core)
+    g.remote_dma(T.peer[:, :], T.stage[:, :], sem.peer_in, sem.sent, pid, rid, _bits(_spread(far, E_PEER)))
+    g.wait_ge(sem.sent, E_STAGE * len(transfers) + E_PEER)
+
+    bound = float(T.tables["BOUND"])
+    sigma = math.sqrt(BETA) / bound
+    ratio = 16.0 ** (1.0 / (N2 + 1))
+    rho = ratio ** -0.5
+    k2 = 2.0 / (1.0 + ratio)
+    kap = math.sqrt(k2)
+    c = k2 / BETA
+    a2, a1, a0 = 3.0 * c * c * kap / 8.0, -5.0 * c * kap / 4.0, 15.0 * kap / 8.0
+
+    V = g.vector
+    n = [0]
+
+    def done(ins):
+        ins.then_inc(sem.vq, 1)
+        n[0] += 1
+
+    def sync():
+        V.wait_ge(sem.vq, n[0])
+
+    col = lambda k: T.col[:, k:k + 1]
+    q, y0, q2, y1, u, a, b, w = [col(k) for k in range(8)]
+    th1, th2 = T.th[:, 0:N1], T.th[:, 64:64 + N2]
+    f1, f2 = T.fac[:, 0:N1], T.fac[:, 64:64 + N2]
+
+    done(V.memset(T.fill[:, 0:N1], 4.0))
+    done(V.memset(T.fill[:, 64:64 + N2], math.sqrt(ratio)))
+    sync()
+    done(V.tensor_tensor_scan(th1, T.fill[:, 0:N1], T.fill[:, 0:N1], BETA, mult, mult))
+    done(V.tensor_tensor_scan(th2, T.fill[:, 64:64 + N2], T.fill[:, 64:64 + N2], BETA, mult, mult))
+    sync()
+
+    V.wait_ge(sem.ld_own, 16)
+    V.wait_ge(sem.peer_in, E_PEER)
+    done(V.tensor_tensor(T.p[:, :], T.own[:, :], T.peer[:, :], add))
+    sync()
+    V.wait_ge(sem.cross_in, E_CROSS)
+    done(V.tensor_tensor(T.s[:, :], T.p[:, :], T.cross[:, :], add))
+    g.scalar.wait_ge(sem.vq, n[0])
+    g.scalar.activation(T.sq[:, :], T.s[:, :], ActivationFunctionType.Square, scale=sigma, accum_out=q).then_inc(sem.aq, 1)
+    sync()
+    V.wait_ge(sem.aq, 1)
+
+    done(V.tensor_scalar(f1, th1, q, 0.25, AluOpType.is_gt, AluOpType.max))
+    sync()
+    done(V.tensor_reduce(y0, f1, AxisListType.X, mult))
+    sync()
+    done(V.tensor_scalar(q2, q, y0, y0, mult, mult))
+    sync()
+    done(V.tensor_scalar(f2, th2, q2, rho, AluOpType.is_gt, AluOpType.max))
+    sync()
+    done(V.tensor_reduce(y1, f2, AxisListType.X, mult))
+    sync()
+    done(V.tensor_scalar(u, q2, y1, y1, mult, mult))
+    sync()
+    done(V.tensor_scalar(a, u, a2, a1, mult, add))
+    sync()
+    done(V.tensor_scalar(b, a, u, a0, mult, add))
+    sync()
+    done(V.tensor_scalar(w, b, y1, 1.0, mult, AluOpType.min))
+    sync()
+    done(V.tensor_scalar(T.yb[:, :], T.s[:, BLK * rank:BLK * rank + BLK], w, y0, mult, mult))
+
+    g.sync.wait_ge(sem.vq, n[0])
+    g.sync.dma_start(T.y[:, :], T.yb[:, :]).then_inc(sem.st, 16)
+    g.sync.wait_ge(sem.st, 16)

@@ -5,6 +5,7 @@ from concourse.mybir import AluOpType, AxisListType, ActivationFunctionType
 P, WID, BLK = 128, 128, 32
 N1, N2 = 43, 63
 BETA = 2.0 ** -48
+RATIO = 16.0 ** (1.0 / (N2 + 1))
 E_STAGE = 4
 E_PEER = 8
 E_CROSS = 8
@@ -17,14 +18,14 @@ SCRATCH = {
     "cross": ("sbuf", [P, WID], "float32"),
     "s": ("sbuf", [P, WID], "float32"),
     "sq": ("sbuf", [P, WID], "float32"),
-    "fill": ("sbuf", [P, 128], "float32"),
-    "th": ("sbuf", [P, 128], "float32"),
+    "fill": ("sbuf", [P, N1 + N2], "float32"),
+    "th": ("sbuf", [P, N1 + N2], "float32"),
     "fac": ("sbuf", [P, 128], "float32"),
     "col": ("sbuf", [P, 16], "float32"),
     "yb": ("sbuf", [P, BLK], "float32"),
     "p": ("psum", [P, WID], "float32"),
 }
-SEMAPHORES = ["ld_stage", "ld_own", "sent", "hin", "peer_in", "cross_in", "vq", "aq", "st"]
+SEMAPHORES = ["ld_stage", "ld_own", "sent", "hin", "peer_in", "cross_in", "th_in", "vq", "aq", "st"]
 
 
 def _engines(mask):
@@ -55,13 +56,21 @@ def _plan(T, topo):
 
 
 def _relay_program(g, core, T, topo, srcs, dst):
-    g.wait_ge(T.sem.hin, E_STAGE * len(srcs))
+    sem, V, mult = T.sem, g.vector, AluOpType.mult
     rid, pid = topo.addr(dst, core)
     m = _bits(_spread(_engines(topo.mask(core, dst)), E_CROSS))
-    g.remote_dma_fused([RemoteDMATransfer(dst_ids=[DstId(rid=rid, pnc=pid)], dma_engine_mask=m, remote_sem=T.sem.cross_in,
+    V.memset(T.fill[:, 0:N1], 4.0).then_inc(sem.vq, 1)
+    V.memset(T.fill[:, N1:N1 + N2], math.sqrt(RATIO)).then_inc(sem.vq, 1)
+    V.wait_ge(sem.vq, 2)
+    V.tensor_tensor_scan(T.th[:, 0:N1], T.fill[:, 0:N1], T.fill[:, 0:N1], BETA, mult, mult).then_inc(sem.vq, 1)
+    V.tensor_tensor_scan(T.th[:, N1:N1 + N2], T.fill[:, N1:N1 + N2], T.fill[:, N1:N1 + N2], BETA, mult, mult).then_inc(sem.vq, 1)
+    g.wait_ge(sem.vq, 4)
+    g.remote_dma(T.th[:, :], T.th[:, :], sem.th_in, sem.sent, pid, rid, m)
+    g.wait_ge(sem.hin, E_STAGE * len(srcs))
+    g.remote_dma_fused([RemoteDMATransfer(dst_ids=[DstId(rid=rid, pnc=pid)], dma_engine_mask=m, remote_sem=sem.cross_in,
                                           srcs=[T.hin[k] for k in range(len(srcs))], dsts=[T.cross[:, :]], alu_op=1)],
-                       local_sem=T.sem.sent)
-    g.wait_ge(T.sem.sent, E_CROSS)
+                       local_sem=sem.sent)
+    g.wait_ge(sem.sent, 2 * E_CROSS)
 
 
 def rank_program(g, core, T, topo):
@@ -100,9 +109,8 @@ def rank_program(g, core, T, topo):
 
     bound = float(T.tables["BOUND"])
     sigma = math.sqrt(BETA) / bound
-    ratio = 16.0 ** (1.0 / (N2 + 1))
-    rho = ratio ** -0.5
-    k2 = 2.0 / (1.0 + ratio)
+    rho = RATIO ** -0.5
+    k2 = 2.0 / (1.0 + RATIO)
     kap = math.sqrt(k2)
     c = k2 / BETA
     a2, a1, a0 = 3.0 * c * c * kap / 8.0, -5.0 * c * kap / 4.0, 15.0 * kap / 8.0
@@ -119,16 +127,10 @@ def rank_program(g, core, T, topo):
 
     col = lambda k: T.col[:, k:k + 1]
     q, y0, q2, y1, u, a, b, w = [col(k) for k in range(8)]
-    th1, th2 = T.th[:, 0:N1], T.th[:, 64:64 + N2]
+    th1, th2 = T.th[:, 0:N1], T.th[:, N1:N1 + N2]
     f1, f2 = T.fac[:, 0:N1], T.fac[:, 64:64 + N2]
 
-    done(V.memset(T.fill[:, 0:N1], 4.0))
-    done(V.memset(T.fill[:, 64:64 + N2], math.sqrt(ratio)))
-    sync()
-    done(V.tensor_tensor_scan(th1, T.fill[:, 0:N1], T.fill[:, 0:N1], BETA, mult, mult))
-    done(V.tensor_tensor_scan(th2, T.fill[:, 64:64 + N2], T.fill[:, 64:64 + N2], BETA, mult, mult))
-    sync()
-
+    V.wait_ge(sem.th_in, E_CROSS)
     V.wait_ge(sem.ld_own, 16)
     V.wait_ge(sem.peer_in, E_PEER)
     done(V.tensor_tensor(T.p[:, :], T.own[:, :], T.peer[:, :], add))

@@ -4,9 +4,11 @@ from concourse.mybir import AluOpType, AxisListType, ActivationFunctionType
 
 P, WID, BLK = 128, 128, 32
 N1, N2 = 43, 63
+CUT = 24
 BETA = 2.0 ** -48
 RATIO = 16.0 ** (1.0 / (N2 + 1))
 E_STAGE = 4
+E_LAD = 4
 E_PEER = 8
 E_CROSS = 8
 
@@ -18,14 +20,15 @@ SCRATCH = {
     "cross": ("sbuf", [P, WID], "float32"),
     "s": ("sbuf", [P, WID], "float32"),
     "sq": ("sbuf", [P, WID], "float32"),
-    "fill": ("sbuf", [P, N1 + N2], "float32"),
-    "th": ("sbuf", [P, N1 + N2], "float32"),
+    "fill": ("sbuf", [P, 64], "float32"),
+    "th1": ("sbuf", [P, N1], "float32"),
+    "th2": ("sbuf", [P, N2], "float32"),
     "fac": ("sbuf", [P, 128], "float32"),
     "col": ("sbuf", [P, 16], "float32"),
     "yb": ("sbuf", [P, BLK], "float32"),
     "p": ("psum", [P, WID], "float32"),
 }
-SEMAPHORES = ["ld_stage", "ld_own", "sent", "hin", "peer_in", "cross_in", "th_in", "vq", "aq", "st"]
+SEMAPHORES = ["ld_stage", "ld_own", "sent", "hin", "peer_in", "cross_in", "th1_in", "th2_in", "tq", "vq", "aq", "st"]
 
 
 def _engines(mask):
@@ -51,22 +54,26 @@ def _plan(T, topo):
             relay = [c for c in range(ncores)
                      if c not in ranks and topo.host(c) == topo.host(src) and topo.chip(c) == topo.chip(src)
                      and topo.die(c) == topo.die(src) and topo.may_write(c, dsts[i])][0]
-            jobs.append((relay, srcs, dsts[i]))
+            jobs.append((relay, src, srcs, dsts[i]))
     return ga, gb, jobs
 
 
-def _relay_program(g, core, T, topo, srcs, dst):
-    sem, V, mult = T.sem, g.vector, AluOpType.mult
-    rid, pid = topo.addr(dst, core)
+def _ladder(g, T, out, width, root, first):
+    V = g.vector
+    V.memset(T.fill[:, 0:width], root).then_inc(T.sem.vq, 1)
+    V.wait_ge(T.sem.vq, 1)
+    V.tensor_tensor_scan(out, T.fill[:, 0:width], T.fill[:, 0:width], first, AluOpType.mult, AluOpType.mult).then_inc(T.sem.tq, 1)
+
+
+def _relay_program(g, core, T, topo, home, srcs, dst):
+    sem = T.sem
     m = _bits(_spread(_engines(topo.mask(core, dst)), E_CROSS))
-    V.memset(T.fill[:, 0:N1], 4.0).then_inc(sem.vq, 1)
-    V.memset(T.fill[:, N1:N1 + N2], math.sqrt(RATIO)).then_inc(sem.vq, 1)
-    V.wait_ge(sem.vq, 2)
-    V.tensor_tensor_scan(T.th[:, 0:N1], T.fill[:, 0:N1], T.fill[:, 0:N1], BETA, mult, mult).then_inc(sem.vq, 1)
-    V.tensor_tensor_scan(T.th[:, N1:N1 + N2], T.fill[:, N1:N1 + N2], T.fill[:, N1:N1 + N2], BETA, mult, mult).then_inc(sem.vq, 1)
-    g.wait_ge(sem.vq, 4)
-    g.remote_dma(T.th[:, :], T.th[:, :], sem.th_in, sem.sent, pid, rid, m)
+    _ladder(g, T, T.th2[:, :], N2, math.sqrt(RATIO), BETA)
+    g.wait_ge(sem.tq, 1)
+    rid, pid = topo.addr(home, core)
+    g.remote_dma(T.th2[:, :], T.th2[:, :], sem.th2_in, sem.sent, pid, rid, m)
     g.wait_ge(sem.hin, E_STAGE * len(srcs))
+    rid, pid = topo.addr(dst, core)
     g.remote_dma_fused([RemoteDMATransfer(dst_ids=[DstId(rid=rid, pnc=pid)], dma_engine_mask=m, remote_sem=sem.cross_in,
                                           srcs=[T.hin[k] for k in range(len(srcs))], dsts=[T.cross[:, :]], alu_op=1)],
                        local_sem=sem.sent)
@@ -75,9 +82,9 @@ def _relay_program(g, core, T, topo, srcs, dst):
 
 def rank_program(g, core, T, topo):
     ga, gb, jobs = _plan(T, topo)
-    for relay, srcs, dst in jobs:
+    for relay, home, srcs, dst in jobs:
         if relay == core:
-            _relay_program(g, core, T, topo, srcs, dst)
+            _relay_program(g, core, T, topo, home, srcs, dst)
             return
     rank = T.rank_of(core)
     if rank is None:
@@ -86,26 +93,30 @@ def rank_program(g, core, T, topo):
     group = ga if core in ga else gb
     partner = [r for r in group if r != core][0]
     mult, add = AluOpType.mult, AluOpType.add
+    V = g.vector
 
     g.sync.dma_start(T.stage[:, :], T.gr[:, :]).then_inc(sem.ld_stage, 16)
     g.sync.dma_start(T.own[:, :], T.gr[:, :]).then_inc(sem.ld_own, 16)
 
     far = _engines(topo.mask(core, partner))
+    prid, ppid = topo.addr(partner, core)
+    lo, hi = (0, CUT) if group.index(core) == 0 else (CUT, N1)
+    _ladder(g, T, T.th1[:, lo:hi], hi - lo, 4.0, BETA * 16.0 ** lo)
+    g.wait_ge(sem.tq, 1)
+    g.remote_dma(T.th1[:, lo:hi], T.th1[:, lo:hi], sem.th1_in, sem.sent, ppid, prid, _bits(far[1::2][:E_LAD]))
+
+    feeds = [(relay, srcs) for relay, home, srcs, dst in jobs if core in srcs]
     transfers = []
-    for relay, srcs, dst in jobs:
-        if core not in srcs:
-            continue
-        avail = _engines(topo.mask(core, relay))
-        near_only = [e for e in avail if e not in far]
-        eng = _spread(near_only if near_only else avail, E_STAGE)
+    for relay, srcs in feeds:
+        near_only = [e for e in _engines(topo.mask(core, relay)) if e not in far]
+        eng = _spread(near_only, E_STAGE) if near_only else far[0::2][:E_STAGE]
         rid, pid = topo.addr(relay, core)
         transfers.append(RemoteDMATransfer(dst_ids=[DstId(rid=rid, pnc=pid)], dma_engine_mask=_bits(eng), remote_sem=sem.hin,
                                            src=T.stage[:, :], dst=T.hin[srcs.index(core)]))
     g.wait_ge(sem.ld_stage, 16)
     g.remote_dma_fused(transfers, local_sem=sem.sent)
-    rid, pid = topo.addr(partner, core)
-    g.remote_dma(T.peer[:, :], T.stage[:, :], sem.peer_in, sem.sent, pid, rid, _bits(_spread(far, E_PEER)))
-    g.wait_ge(sem.sent, E_STAGE * len(transfers) + E_PEER)
+    g.remote_dma(T.peer[:, :], T.stage[:, :], sem.peer_in, sem.sent, ppid, prid, _bits(_spread(far, E_PEER)))
+    g.wait_ge(sem.sent, E_STAGE * len(transfers) + E_PEER + E_LAD)
 
     bound = float(T.tables["BOUND"])
     sigma = math.sqrt(BETA) / bound
@@ -115,8 +126,7 @@ def rank_program(g, core, T, topo):
     c = k2 / BETA
     a2, a1, a0 = 3.0 * c * c * kap / 8.0, -5.0 * c * kap / 4.0, 15.0 * kap / 8.0
 
-    V = g.vector
-    n = [0]
+    n = [1]
 
     def done(ins):
         ins.then_inc(sem.vq, 1)
@@ -127,13 +137,17 @@ def rank_program(g, core, T, topo):
 
     col = lambda k: T.col[:, k:k + 1]
     q, y0, q2, y1, u, a, b, w = [col(k) for k in range(8)]
-    th1, th2 = T.th[:, 0:N1], T.th[:, N1:N1 + N2]
+    th1, th2 = T.th1[:, :], T.th2[:, :]
     f1, f2 = T.fac[:, 0:N1], T.fac[:, 64:64 + N2]
 
-    V.wait_ge(sem.th_in, E_CROSS)
+    V.wait_ge(sem.tq, 1)
     V.wait_ge(sem.ld_own, 16)
+    done(V.tensor_copy(T.p[:, :], T.own[:, :]))
+    sync()
+    V.wait_ge(sem.th1_in, E_LAD)
+    V.wait_ge(sem.th2_in, E_CROSS)
     V.wait_ge(sem.peer_in, E_PEER)
-    done(V.tensor_tensor(T.p[:, :], T.own[:, :], T.peer[:, :], add))
+    done(V.tensor_tensor(T.p[:, :], T.p[:, :], T.peer[:, :], add))
     sync()
     V.wait_ge(sem.cross_in, E_CROSS)
     done(V.tensor_tensor(T.s[:, :], T.p[:, :], T.cross[:, :], add))

@@ -3,12 +3,17 @@ from concourse.bass import DstId, RemoteDMATransfer
 from concourse.mybir import AluOpType, AxisListType, ActivationFunctionType
 
 P, WID, BLK = 128, 128, 32
-N1, N2 = 43, 63
-CUT = 24
-BETA = 2.0 ** -48
-RATIO = 16.0 ** (1.0 / (N2 + 1))
-E_STAGE = 4
-E_LAD = 4
+N1 = 64
+PARTS = ((0, 16), (16, 32))
+REST = (32, N1)
+BETA = 2.0 / 3.0
+COEF = (0.6324555308254532, -0.18973522061696357, 0.08538074887001218, -0.04273061593083155, 0.022434776642144653,
+        -0.011793103689249133, 0.006480965165908961, -0.004712995992872147, 0.002661338317453305,
+        0.00032787391342725317, -0.00019614814930089429, -0.0013557674981520861, 0.0007826876660595665)
+DEG = len(COEF) - 1
+E_NEAR = 4
+E_FAR = 8
+E_LAD = 8
 E_PEER = 8
 E_CROSS = 8
 
@@ -22,8 +27,11 @@ SCRATCH = {
     "sq": ("sbuf", [P, WID], "float32"),
     "fill": ("sbuf", [P, 64], "float32"),
     "th1": ("sbuf", [P, N1], "float32"),
-    "th2": ("sbuf", [P, N2], "float32"),
-    "fac": ("sbuf", [P, 128], "float32"),
+    "fac": ("sbuf", [P, N1], "float32"),
+    "sh": ("sbuf", [P, DEG], "float32"),
+    "cf": ("sbuf", [P, DEG], "float32"),
+    "xt": ("sbuf", [P, DEG], "float32"),
+    "pv": ("sbuf", [P, DEG], "float32"),
     "col": ("sbuf", [P, 16], "float32"),
     "yb": ("sbuf", [P, BLK], "float32"),
     "p": ("psum", [P, WID], "float32"),
@@ -58,21 +66,23 @@ def _plan(T, topo):
     return ga, gb, jobs
 
 
-def _ladder(g, T, out, width, root, first):
+def _ladder(g, T, lo, hi):
     V = g.vector
-    V.memset(T.fill[:, 0:width], root).then_inc(T.sem.vq, 1)
+    V.memset(T.fill[:, 0:hi - lo], 2.0).then_inc(T.sem.vq, 1)
     V.wait_ge(T.sem.vq, 1)
-    V.tensor_tensor_scan(out, T.fill[:, 0:width], T.fill[:, 0:width], first, AluOpType.mult, AluOpType.mult).then_inc(T.sem.tq, 1)
+    V.tensor_tensor_scan(T.th1[:, lo:hi], T.fill[:, 0:hi - lo], T.fill[:, 0:hi - lo], BETA * 4.0 ** lo,
+                         AluOpType.mult, AluOpType.mult).then_inc(T.sem.tq, 1)
 
 
 def _relay_program(g, core, T, topo, home, srcs, dst):
     sem = T.sem
     m = _bits(_spread(_engines(topo.mask(core, dst)), E_CROSS))
-    _ladder(g, T, T.th2[:, :], N2, math.sqrt(RATIO), BETA)
+    lo, hi = REST
+    _ladder(g, T, lo, hi)
     g.wait_ge(sem.tq, 1)
     rid, pid = topo.addr(home, core)
-    g.remote_dma(T.th2[:, :], T.th2[:, :], sem.th2_in, sem.sent, pid, rid, m)
-    g.wait_ge(sem.hin, E_STAGE * len(srcs))
+    g.remote_dma(T.th1[:, lo:hi], T.th1[:, lo:hi], sem.th2_in, sem.sent, pid, rid, m)
+    g.wait_ge(sem.hin, E_NEAR + E_FAR)
     rid, pid = topo.addr(dst, core)
     g.remote_dma_fused([RemoteDMATransfer(dst_ids=[DstId(rid=rid, pnc=pid)], dma_engine_mask=m, remote_sem=sem.cross_in,
                                           srcs=[T.hin[k] for k in range(len(srcs))], dsts=[T.cross[:, :]], alu_op=1)],
@@ -100,31 +110,25 @@ def rank_program(g, core, T, topo):
 
     far = _engines(topo.mask(core, partner))
     prid, ppid = topo.addr(partner, core)
-    lo, hi = (0, CUT) if group.index(core) == 0 else (CUT, N1)
-    _ladder(g, T, T.th1[:, lo:hi], hi - lo, 4.0, BETA * 16.0 ** lo)
+    lo, hi = PARTS[group.index(core)]
+    _ladder(g, T, lo, hi)
     g.wait_ge(sem.tq, 1)
-    g.remote_dma(T.th1[:, lo:hi], T.th1[:, lo:hi], sem.th1_in, sem.sent, ppid, prid, _bits(far[1::2][:E_LAD]))
+    g.remote_dma(T.th1[:, lo:hi], T.th1[:, lo:hi], sem.th1_in, sem.sent, ppid, prid, _bits(_spread(far, E_LAD)))
 
     feeds = [(relay, srcs) for relay, home, srcs, dst in jobs if core in srcs]
     transfers = []
     for relay, srcs in feeds:
         near_only = [e for e in _engines(topo.mask(core, relay)) if e not in far]
-        eng = _spread(near_only, E_STAGE) if near_only else far[0::2][:E_STAGE]
+        eng = _spread(near_only, E_NEAR) if near_only else _spread(far, E_FAR)
         rid, pid = topo.addr(relay, core)
         transfers.append(RemoteDMATransfer(dst_ids=[DstId(rid=rid, pnc=pid)], dma_engine_mask=_bits(eng), remote_sem=sem.hin,
                                            src=T.stage[:, :], dst=T.hin[srcs.index(core)]))
     g.wait_ge(sem.ld_stage, 16)
     g.remote_dma_fused(transfers, local_sem=sem.sent)
     g.remote_dma(T.peer[:, :], T.stage[:, :], sem.peer_in, sem.sent, ppid, prid, _bits(_spread(far, E_PEER)))
-    g.wait_ge(sem.sent, E_STAGE * len(transfers) + E_PEER + E_LAD)
+    g.wait_ge(sem.sent, E_NEAR + E_FAR + E_PEER + E_LAD)
 
-    bound = float(T.tables["BOUND"])
-    sigma = math.sqrt(BETA) / bound
-    rho = RATIO ** -0.5
-    k2 = 2.0 / (1.0 + RATIO)
-    kap = math.sqrt(k2)
-    c = k2 / BETA
-    a2, a1, a0 = 3.0 * c * c * kap / 8.0, -5.0 * c * kap / 4.0, 15.0 * kap / 8.0
+    sigma = math.sqrt(BETA) / float(T.tables["BOUND"])
 
     n = [1]
 
@@ -136,11 +140,13 @@ def rank_program(g, core, T, topo):
         V.wait_ge(sem.vq, n[0])
 
     col = lambda k: T.col[:, k:k + 1]
-    q, y0, q2, y1, u, a, b, w = [col(k) for k in range(8)]
-    th1, th2 = T.th1[:, :], T.th2[:, :]
-    f1, f2 = T.fac[:, 0:N1], T.fac[:, 64:64 + N2]
+    q, y0, q2 = [col(k) for k in range(3)]
 
     V.wait_ge(sem.tq, 1)
+    done(V.memset(T.sh[:, :], -5.0 / 3.0))
+    for t in range(DEG):
+        done(V.memset(T.cf[:, t:t + 1], COEF[DEG - 1 - t]))
+
     V.wait_ge(sem.ld_own, 16)
     done(V.tensor_copy(T.p[:, :], T.own[:, :]))
     sync()
@@ -156,25 +162,17 @@ def rank_program(g, core, T, topo):
     sync()
     V.wait_ge(sem.aq, 1)
 
-    done(V.tensor_scalar(f1, th1, q, 0.25, AluOpType.is_gt, AluOpType.max))
+    done(V.tensor_scalar(T.fac[:, :], T.th1[:, :], q, 0.5, AluOpType.is_gt, AluOpType.max))
     sync()
-    done(V.tensor_reduce(y0, f1, AxisListType.X, mult))
+    done(V.tensor_reduce(y0, T.fac[:, :], AxisListType.X, mult))
     sync()
     done(V.tensor_scalar(q2, q, y0, y0, mult, mult))
     sync()
-    done(V.tensor_scalar(f2, th2, q2, rho, AluOpType.is_gt, AluOpType.max))
+    done(V.tensor_scalar(T.xt[:, :], T.sh[:, :], q2, -1.0, add, AluOpType.max))
     sync()
-    done(V.tensor_reduce(y1, f2, AxisListType.X, mult))
+    done(V.tensor_tensor_scan(T.pv[:, :], T.xt[:, :], T.cf[:, :], COEF[DEG], mult, add))
     sync()
-    done(V.tensor_scalar(u, q2, y1, y1, mult, mult))
-    sync()
-    done(V.tensor_scalar(a, u, a2, a1, mult, add))
-    sync()
-    done(V.tensor_scalar(b, a, u, a0, mult, add))
-    sync()
-    done(V.tensor_scalar(w, b, y1, 1.0, mult, AluOpType.min))
-    sync()
-    done(V.tensor_scalar(T.yb[:, :], T.s[:, BLK * rank:BLK * rank + BLK], w, y0, mult, mult))
+    done(V.tensor_scalar(T.yb[:, :], T.s[:, BLK * rank:BLK * rank + BLK], T.pv[:, DEG - 1:DEG], y0, mult, mult))
 
     g.sync.wait_ge(sem.vq, n[0])
     g.sync.dma_start(T.y[:, :], T.yb[:, :]).then_inc(sem.st, 16)

@@ -11,6 +11,8 @@ COEF = (0.6324555308254532, -0.18973522061696357, 0.08538074887001218, -0.042730
         -0.011793103689249133, 0.006480965165908961, -0.004712995992872147, 0.002661338317453305,
         0.00032787391342725317, -0.00019614814930089429, -0.0013557674981520861, 0.0007826876660595665)
 DEG = len(COEF) - 1
+QC = 2 * N1
+W = QC + 1 + DEG
 E_NEAR = 4
 E_FAR = 8
 E_LAD = 8
@@ -27,12 +29,12 @@ SCRATCH = {
     "sq": ("sbuf", [P, WID], "float32"),
     "fill": ("sbuf", [P, 64], "float32"),
     "th1": ("sbuf", [P, N1], "float32"),
-    "fac": ("sbuf", [P, N1], "float32"),
-    "sh": ("sbuf", [P, DEG], "float32"),
+    "th": ("sbuf", [P, QC], "float32"),
+    "d0": ("sbuf", [P, W], "float32"),
+    "d1": ("sbuf", [P, W], "float32"),
+    "sc": ("sbuf", [P, W], "float32"),
     "cf": ("sbuf", [P, DEG], "float32"),
-    "xt": ("sbuf", [P, DEG], "float32"),
     "pv": ("sbuf", [P, DEG], "float32"),
-    "col": ("sbuf", [P, 16], "float32"),
     "yb": ("sbuf", [P, BLK], "float32"),
     "p": ("psum", [P, WID], "float32"),
 }
@@ -103,7 +105,7 @@ def rank_program(g, core, T, topo):
     group = ga if core in ga else gb
     partner = [r for r in group if r != core][0]
     mult, add = AluOpType.mult, AluOpType.add
-    V = g.vector
+    V, A = g.vector, g.scalar
 
     g.sync.dma_start(T.stage[:, :], T.gr[:, :]).then_inc(sem.ld_stage, 16)
     g.sync.dma_start(T.own[:, :], T.gr[:, :]).then_inc(sem.ld_own, 16)
@@ -139,40 +141,43 @@ def rank_program(g, core, T, topo):
     def sync():
         V.wait_ge(sem.vq, n[0])
 
-    col = lambda k: T.col[:, k:k + 1]
-    q, y0, q2 = [col(k) for k in range(3)]
+    q = T.d0[:, QC:QC + 1]
 
     V.wait_ge(sem.tq, 1)
-    done(V.memset(T.sh[:, :], -5.0 / 3.0))
+    done(V.memset(T.d0[:, QC + 1:W], 1.0))
+    done(V.memset(T.d1[:, 0:QC], 0.0))
+    done(V.memset(T.d1[:, QC + 1:QC + 2], -5.0 / 3.0))
+    done(V.memset(T.d1[:, QC + 2:W], 0.0))
     for t in range(DEG):
         done(V.memset(T.cf[:, t:t + 1], COEF[DEG - 1 - t]))
 
     V.wait_ge(sem.ld_own, 16)
     done(V.tensor_copy(T.p[:, :], T.own[:, :]))
-    sync()
     V.wait_ge(sem.th1_in, E_LAD)
     V.wait_ge(sem.th2_in, E_CROSS)
+    done(V.tensor_copy(T.th[:, 0:N1], T.th1[:, :]))
+    done(V.tensor_copy(T.th[:, N1:QC], T.th1[:, :]))
+    sync()
     V.wait_ge(sem.peer_in, E_PEER)
     done(V.tensor_tensor(T.p[:, :], T.p[:, :], T.peer[:, :], add))
     sync()
     V.wait_ge(sem.cross_in, E_CROSS)
     done(V.tensor_tensor(T.s[:, :], T.p[:, :], T.cross[:, :], add))
-    g.scalar.wait_ge(sem.vq, n[0])
-    g.scalar.activation(T.sq[:, :], T.s[:, :], ActivationFunctionType.Square, scale=sigma, accum_out=q).then_inc(sem.aq, 1)
+    A.wait_ge(sem.vq, n[0])
+    A.activation(T.sq[:, :], T.s[:, :], ActivationFunctionType.Square, scale=sigma, accum_out=q).then_inc(sem.aq, 1)
+    A.wait_ge(sem.aq, 1)
+    A.activation(T.d1[:, QC:QC + 1], q, ActivationFunctionType.Relu, bias=BETA, scale=-1.0).then_inc(sem.aq, 1)
     sync()
     V.wait_ge(sem.aq, 1)
 
-    done(V.tensor_scalar(T.fac[:, :], T.th1[:, :], q, 0.5, AluOpType.is_gt, AluOpType.max))
+    done(V.tensor_scalar(T.d0[:, 0:QC], T.th[:, :], q, 0.5, AluOpType.is_gt, AluOpType.max))
     sync()
-    done(V.tensor_reduce(y0, T.fac[:, :], AxisListType.X, mult))
+    V.wait_ge(sem.aq, 2)
+    done(V.tensor_tensor_scan(T.sc[:, :], T.d0[:, :], T.d1[:, :], 1.0, mult, add))
     sync()
-    done(V.tensor_scalar(q2, q, y0, y0, mult, mult))
+    done(V.tensor_tensor_scan(T.pv[:, :], T.sc[:, QC + 1:W], T.cf[:, :], COEF[DEG], mult, add))
     sync()
-    done(V.tensor_scalar(T.xt[:, :], T.sh[:, :], q2, -1.0, add, AluOpType.max))
-    sync()
-    done(V.tensor_tensor_scan(T.pv[:, :], T.xt[:, :], T.cf[:, :], COEF[DEG], mult, add))
-    sync()
-    done(V.tensor_scalar(T.yb[:, :], T.s[:, BLK * rank:BLK * rank + BLK], T.pv[:, DEG - 1:DEG], y0, mult, mult))
+    done(V.tensor_scalar(T.yb[:, :], T.s[:, BLK * rank:BLK * rank + BLK], T.pv[:, DEG - 1:DEG], T.sc[:, N1 - 1:N1], mult, mult))
 
     g.sync.wait_ge(sem.vq, n[0])
     g.sync.dma_start(T.y[:, :], T.yb[:, :]).then_inc(sem.st, 16)

@@ -1,11 +1,11 @@
 import math
-from concourse.bass import DstId, RemoteDMATransfer
 from concourse.mybir import AluOpType, AxisListType, ActivationFunctionType
 
 P, WID, BLK = 128, 128, 32
 N1 = 64
 PARTS = ((0, 16), (16, 32))
-REST = (32, N1)
+REST = ((32, 48), (48, N1))
+FW = 16
 BETA = 2.0 / 3.0
 COEF = (0.6324555308254532, -0.18973522061696357, 0.08538074887001218, -0.04273061593083155, 0.022434776642144653,
         -0.011793103689249133, 0.006480965165908961, -0.004712995992872147, 0.002661338317453305,
@@ -13,21 +13,22 @@ COEF = (0.6324555308254532, -0.18973522061696357, 0.08538074887001218, -0.042730
 DEG = len(COEF) - 1
 QC = 2 * N1
 W = QC + 1 + DEG
-E_NEAR = 4
-E_FAR = 8
+E_HOP = 8
 E_LAD = 8
 E_PEER = 8
 E_CROSS = 8
 
 SCRATCH = {
     "stage": ("dram", [P, WID], "float32"),
-    "hin": ("dram", [2, P, WID], "float32"),
+    "hin": ("dram", [P, WID], "float32"),
     "own": ("sbuf", [P, WID], "float32"),
     "peer": ("sbuf", [P, WID], "float32"),
-    "cross": ("sbuf", [P, WID], "float32"),
+    "cross0": ("sbuf", [P, WID], "float32"),
+    "cross1": ("sbuf", [P, WID], "float32"),
     "s": ("sbuf", [P, WID], "float32"),
     "sq": ("sbuf", [P, WID], "float32"),
-    "fill": ("sbuf", [P, 64], "float32"),
+    "fill": ("sbuf", [P, FW], "float32"),
+    "pfill": ("sbuf", [P, FW], "float32"),
     "th1": ("sbuf", [P, N1], "float32"),
     "th": ("sbuf", [P, QC], "float32"),
     "d0": ("sbuf", [P, W], "float32"),
@@ -38,7 +39,8 @@ SCRATCH = {
     "yb": ("sbuf", [P, BLK], "float32"),
     "p": ("psum", [P, WID], "float32"),
 }
-SEMAPHORES = ["ld_stage", "ld_own", "sent", "hin", "peer_in", "cross_in", "th1_in", "th2_in", "tq", "vq", "aq", "st"]
+SEMAPHORES = ["ld_stage", "ld_own", "sent", "hin", "peer_in", "cross0_in", "cross1_in", "th1_in", "th2_in", "tq", "vq", "aq",
+              "st"]
 
 
 def _engines(mask):
@@ -61,42 +63,41 @@ def _plan(T, topo):
     jobs = []
     for srcs, dsts in ((ga, gb), (gb, ga)):
         for i, src in enumerate(srcs):
-            relay = [c for c in range(ncores)
-                     if c not in ranks and topo.host(c) == topo.host(src) and topo.chip(c) == topo.chip(src)
-                     and topo.die(c) == topo.die(src) and topo.may_write(c, dsts[i])][0]
-            jobs.append((relay, src, srcs, dsts[i]))
+            can = [c for c in range(ncores)
+                   if c not in ranks and topo.host(c) == topo.host(src) and topo.chip(c) == topo.chip(src)
+                   and all(topo.may_write(c, d) for d in dsts)]
+            jobs.append(([c for c in can if topo.die(c) == topo.die(src)][0], src, 0, dsts[i]))
+            jobs.append(([c for c in can if topo.die(c) != topo.die(src)][0], src, 1, dsts[len(dsts) - 1 - i]))
     return ga, gb, jobs
 
 
-def _ladder(g, T, lo, hi):
-    V = g.vector
-    V.memset(T.fill[:, 0:hi - lo], 2.0).then_inc(T.sem.vq, 1)
-    V.wait_ge(T.sem.vq, 1)
-    V.tensor_tensor_scan(T.th1[:, lo:hi], T.fill[:, 0:hi - lo], T.fill[:, 0:hi - lo], BETA * 4.0 ** lo,
-                         AluOpType.mult, AluOpType.mult).then_inc(T.sem.tq, 1)
+def _scan_part(g, T, part, twos):
+    lo, hi = part
+    return g.vector.tensor_tensor_scan(T.th1[:, lo:hi], twos, twos, BETA * 4.0 ** lo, AluOpType.mult, AluOpType.mult)
 
 
-def _relay_program(g, core, T, topo, home, srcs, dst):
+def _relay_program(g, core, T, topo, home, slot, dst):
     sem = T.sem
+    V = g.vector
     m = _bits(_spread(_engines(topo.mask(core, dst)), E_CROSS))
-    lo, hi = REST
-    _ladder(g, T, lo, hi)
+    lo, hi = REST[slot]
+    V.memset(T.fill[:, :], 2.0).then_inc(sem.vq, 1)
+    V.wait_ge(sem.vq, 1)
+    _scan_part(g, T, REST[slot], T.fill[:, :]).then_inc(sem.tq, 1)
     g.wait_ge(sem.tq, 1)
     rid, pid = topo.addr(home, core)
     g.remote_dma(T.th1[:, lo:hi], T.th1[:, lo:hi], sem.th2_in, sem.sent, pid, rid, m)
-    g.wait_ge(sem.hin, E_NEAR + E_FAR)
+    g.wait_ge(sem.hin, E_HOP)
     rid, pid = topo.addr(dst, core)
-    g.remote_dma_fused([RemoteDMATransfer(dst_ids=[DstId(rid=rid, pnc=pid)], dma_engine_mask=m, remote_sem=sem.cross_in,
-                                          srcs=[T.hin[k] for k in range(len(srcs))], dsts=[T.cross[:, :]], alu_op=1)],
-                       local_sem=sem.sent)
+    g.remote_dma(T["cross%d" % slot][:, :], T.hin[:, :], sem["cross%d_in" % slot], sem.sent, pid, rid, m)
     g.wait_ge(sem.sent, 2 * E_CROSS)
 
 
 def rank_program(g, core, T, topo):
     ga, gb, jobs = _plan(T, topo)
-    for relay, home, srcs, dst in jobs:
+    for relay, home, slot, dst in jobs:
         if relay == core:
-            _relay_program(g, core, T, topo, home, srcs, dst)
+            _relay_program(g, core, T, topo, home, slot, dst)
             return
     rank = T.rank_of(core)
     if rank is None:
@@ -112,27 +113,22 @@ def rank_program(g, core, T, topo):
 
     far = _engines(topo.mask(core, partner))
     prid, ppid = topo.addr(partner, core)
-    lo, hi = PARTS[group.index(core)]
-    _ladder(g, T, lo, hi)
+    V.memset(T.fill[:, :], 2.0).then_inc(sem.tq, 1)
     g.wait_ge(sem.tq, 1)
-    g.remote_dma(T.th1[:, lo:hi], T.th1[:, lo:hi], sem.th1_in, sem.sent, ppid, prid, _bits(_spread(far, E_LAD)))
+    g.remote_dma(T.pfill[:, :], T.fill[:, :], sem.th1_in, sem.sent, ppid, prid, _bits(_spread(far, E_LAD)))
 
-    feeds = [(relay, srcs) for relay, home, srcs, dst in jobs if core in srcs]
-    transfers = []
-    for relay, srcs in feeds:
-        near_only = [e for e in _engines(topo.mask(core, relay)) if e not in far]
-        eng = _spread(near_only, E_NEAR) if near_only else _spread(far, E_FAR)
-        rid, pid = topo.addr(relay, core)
-        transfers.append(RemoteDMATransfer(dst_ids=[DstId(rid=rid, pnc=pid)], dma_engine_mask=_bits(eng), remote_sem=sem.hin,
-                                           src=T.stage[:, :], dst=T.hin[srcs.index(core)]))
     g.wait_ge(sem.ld_stage, 16)
-    g.remote_dma_fused(transfers, local_sem=sem.sent)
+    for slot in (1, 0):
+        relay = [r for r, home, sl, dst in jobs if home == core and sl == slot][0]
+        near_only = [e for e in _engines(topo.mask(core, relay)) if e not in far]
+        rid, pid = topo.addr(relay, core)
+        g.remote_dma(T.hin[:, :], T.stage[:, :], sem.hin, sem.sent, pid, rid, _bits(_spread(far if slot else near_only, E_HOP)))
     g.remote_dma(T.peer[:, :], T.stage[:, :], sem.peer_in, sem.sent, ppid, prid, _bits(_spread(far, E_PEER)))
-    g.wait_ge(sem.sent, E_NEAR + E_FAR + E_PEER + E_LAD)
+    g.wait_ge(sem.sent, 2 * E_HOP + E_PEER + E_LAD)
 
     sigma = math.sqrt(BETA) / float(T.tables["BOUND"])
 
-    n = [1]
+    n = [0]
 
     def done(ins):
         ins.then_inc(sem.vq, 1)
@@ -144,6 +140,7 @@ def rank_program(g, core, T, topo):
     q = T.d0[:, QC:QC + 1]
 
     V.wait_ge(sem.tq, 1)
+    done(_scan_part(g, T, PARTS[0], T.fill[:, :]))
     done(V.memset(T.d0[:, QC + 1:W], 1.0))
     done(V.memset(T.d1[:, 0:QC], 0.0))
     done(V.memset(T.d1[:, QC + 1:QC + 2], -5.0 / 3.0))
@@ -154,15 +151,20 @@ def rank_program(g, core, T, topo):
     V.wait_ge(sem.ld_own, 16)
     done(V.tensor_copy(T.p[:, :], T.own[:, :]))
     V.wait_ge(sem.th1_in, E_LAD)
-    V.wait_ge(sem.th2_in, E_CROSS)
+    done(_scan_part(g, T, PARTS[1], T.pfill[:, :]))
+    V.wait_ge(sem.th2_in, 2 * E_CROSS)
+    sync()
     done(V.tensor_copy(T.th[:, 0:N1], T.th1[:, :]))
     done(V.tensor_copy(T.th[:, N1:QC], T.th1[:, :]))
     sync()
     V.wait_ge(sem.peer_in, E_PEER)
     done(V.tensor_tensor(T.p[:, :], T.p[:, :], T.peer[:, :], add))
     sync()
-    V.wait_ge(sem.cross_in, E_CROSS)
-    done(V.tensor_tensor(T.s[:, :], T.p[:, :], T.cross[:, :], add))
+    V.wait_ge(sem.cross1_in, E_CROSS)
+    done(V.tensor_tensor(T.p[:, :], T.p[:, :], T.cross1[:, :], add))
+    sync()
+    V.wait_ge(sem.cross0_in, E_CROSS)
+    done(V.tensor_tensor(T.s[:, :], T.p[:, :], T.cross0[:, :], add))
     A.wait_ge(sem.vq, n[0])
     A.activation(T.sq[:, :], T.s[:, :], ActivationFunctionType.Square, scale=sigma, accum_out=q).then_inc(sem.aq, 1)
     A.wait_ge(sem.aq, 1)

import math
from concourse.mybir import AluOpType, AxisListType, ActivationFunctionType

P, WID, BLK = 128, 128, 32
N1 = 64
PARTS = ((0, 16), (16, 32))
REST = ((32, 48), (48, N1))
FW = 16
BETA = 2.0 / 3.0
COEF = (0.6324555308254532, -0.18973522061696357, 0.08538074887001218, -0.04273061593083155, 0.022434776642144653,
        -0.011793103689249133, 0.006480965165908961, -0.004712995992872147, 0.002661338317453305,
        0.00032787391342725317, -0.00019614814930089429, -0.0013557674981520861, 0.0007826876660595665)
DEG = len(COEF) - 1
QC = 2 * N1
W = QC + 1 + DEG
E_HOP = 8
E_LAD = 8
E_PEER = 8
E_CROSS = 8

SCRATCH = {
    "stage": ("dram", [P, WID], "float32"),
    "hin": ("dram", [P, WID], "float32"),
    "own": ("sbuf", [P, WID], "float32"),
    "peer": ("sbuf", [P, WID], "float32"),
    "cross0": ("sbuf", [P, WID], "float32"),
    "cross1": ("sbuf", [P, WID], "float32"),
    "s": ("sbuf", [P, WID], "float32"),
    "sq": ("sbuf", [P, WID], "float32"),
    "fill": ("sbuf", [P, FW], "float32"),
    "pfill": ("sbuf", [P, FW], "float32"),
    "th1": ("sbuf", [P, N1], "float32"),
    "th": ("sbuf", [P, QC], "float32"),
    "d0": ("sbuf", [P, W], "float32"),
    "d1": ("sbuf", [P, W], "float32"),
    "sc": ("sbuf", [P, W], "float32"),
    "cf": ("sbuf", [P, DEG], "float32"),
    "pv": ("sbuf", [P, DEG], "float32"),
    "yb": ("sbuf", [P, BLK], "float32"),
    "p": ("psum", [P, WID], "float32"),
}
SEMAPHORES = ["ld_stage", "ld_own", "sent", "hin", "peer_in", "cross0_in", "cross1_in", "th1_in", "th2_in", "tq", "vq", "aq",
              "st"]


def _engines(mask):
    return [e for e in range(mask.bit_length()) if (mask >> e) & 1]


def _spread(lst, n):
    return lst[::len(lst) // n][:n]


def _bits(lst):
    return sum(1 << e for e in lst)


def _plan(T, topo):
    ranks = list(T.cores)
    ga = [r for r in ranks if r == ranks[0] or topo.may_write(ranks[0], r)]
    gb = [r for r in ranks if r not in ga]
    ncores = (max(topo.host(r) for r in ranks) + 1) * topo.CORES_PER_HOST
    jobs = []
    for srcs, dsts in ((ga, gb), (gb, ga)):
        for i, src in enumerate(srcs):
            can = [c for c in range(ncores)
                   if c not in ranks and topo.host(c) == topo.host(src) and topo.chip(c) == topo.chip(src)
                   and all(topo.may_write(c, d) for d in dsts)]
            jobs.append(([c for c in can if topo.die(c) == topo.die(src)][0], src, 0, dsts[i]))
            jobs.append(([c for c in can if topo.die(c) != topo.die(src)][0], src, 1, dsts[len(dsts) - 1 - i]))
    return ga, gb, jobs


def _scan_part(g, T, part, twos):
    lo, hi = part
    return g.vector.tensor_tensor_scan(T.th1[:, lo:hi], twos, twos, BETA * 4.0 ** lo, AluOpType.mult, AluOpType.mult)


def _relay_program(g, core, T, topo, home, slot, dst):
    sem = T.sem
    V = g.vector
    m = _bits(_spread(_engines(topo.mask(core, dst)), E_CROSS))
    lo, hi = REST[slot]
    V.memset(T.fill[:, :], 2.0).then_inc(sem.vq, 1)
    V.wait_ge(sem.vq, 1)
    _scan_part(g, T, REST[slot], T.fill[:, :]).then_inc(sem.tq, 1)
    g.wait_ge(sem.tq, 1)
    rid, pid = topo.addr(home, core)
    g.remote_dma(T.th1[:, lo:hi], T.th1[:, lo:hi], sem.th2_in, sem.sent, pid, rid, m)
    g.wait_ge(sem.hin, E_HOP)
    rid, pid = topo.addr(dst, core)
    g.remote_dma(T["cross%d" % slot][:, :], T.hin[:, :], sem["cross%d_in" % slot], sem.sent, pid, rid, m)
    g.wait_ge(sem.sent, 2 * E_CROSS)


def rank_program(g, core, T, topo):
    ga, gb, jobs = _plan(T, topo)
    for relay, home, slot, dst in jobs:
        if relay == core:
            _relay_program(g, core, T, topo, home, slot, dst)
            return
    rank = T.rank_of(core)
    if rank is None:
        return
    sem = T.sem
    group = ga if core in ga else gb
    partner = [r for r in group if r != core][0]
    mult, add = AluOpType.mult, AluOpType.add
    V, A = g.vector, g.scalar

    g.sync.dma_start(T.stage[:, :], T.gr[:, :]).then_inc(sem.ld_stage, 16)
    g.sync.dma_start(T.own[:, :], T.gr[:, :]).then_inc(sem.ld_own, 16)

    far = _engines(topo.mask(core, partner))
    prid, ppid = topo.addr(partner, core)
    V.memset(T.fill[:, :], 2.0).then_inc(sem.tq, 1)
    g.wait_ge(sem.tq, 1)
    g.remote_dma(T.pfill[:, :], T.fill[:, :], sem.th1_in, sem.sent, ppid, prid, _bits(_spread(far, E_LAD)))

    g.wait_ge(sem.ld_stage, 16)
    for slot in (1, 0):
        relay = [r for r, home, sl, dst in jobs if home == core and sl == slot][0]
        near_only = [e for e in _engines(topo.mask(core, relay)) if e not in far]
        rid, pid = topo.addr(relay, core)
        g.remote_dma(T.hin[:, :], T.stage[:, :], sem.hin, sem.sent, pid, rid, _bits(_spread(far if slot else near_only, E_HOP)))
    g.remote_dma(T.peer[:, :], T.stage[:, :], sem.peer_in, sem.sent, ppid, prid, _bits(_spread(far, E_PEER)))
    g.wait_ge(sem.sent, 2 * E_HOP + E_PEER + E_LAD)

    sigma = math.sqrt(BETA) / float(T.tables["BOUND"])

    n = [0]

    def done(ins):
        ins.then_inc(sem.vq, 1)
        n[0] += 1

    def sync():
        V.wait_ge(sem.vq, n[0])

    q = T.d0[:, QC:QC + 1]

    V.wait_ge(sem.tq, 1)
    done(_scan_part(g, T, PARTS[0], T.fill[:, :]))
    done(V.memset(T.d0[:, QC + 1:W], 1.0))
    done(V.memset(T.d1[:, 0:QC], 0.0))
    done(V.memset(T.d1[:, QC + 1:QC + 2], -5.0 / 3.0))
    done(V.memset(T.d1[:, QC + 2:W], 0.0))
    for t in range(DEG):
        done(V.memset(T.cf[:, t:t + 1], COEF[DEG - 1 - t]))

    V.wait_ge(sem.ld_own, 16)
    done(V.tensor_copy(T.p[:, :], T.own[:, :]))
    V.wait_ge(sem.th1_in, E_LAD)
    done(_scan_part(g, T, PARTS[1], T.pfill[:, :]))
    V.wait_ge(sem.th2_in, 2 * E_CROSS)
    sync()
    done(V.tensor_copy(T.th[:, 0:N1], T.th1[:, :]))
    done(V.tensor_copy(T.th[:, N1:QC], T.th1[:, :]))
    sync()
    V.wait_ge(sem.peer_in, E_PEER)
    done(V.tensor_tensor(T.p[:, :], T.p[:, :], T.peer[:, :], add))
    sync()
    V.wait_ge(sem.cross1_in, E_CROSS)
    done(V.tensor_tensor(T.p[:, :], T.p[:, :], T.cross1[:, :], add))
    sync()
    V.wait_ge(sem.cross0_in, E_CROSS)
    done(V.tensor_tensor(T.s[:, :], T.p[:, :], T.cross0[:, :], add))
    A.wait_ge(sem.vq, n[0])
    A.activation(T.sq[:, :], T.s[:, :], ActivationFunctionType.Square, scale=sigma, accum_out=q).then_inc(sem.aq, 1)
    A.wait_ge(sem.aq, 1)
    A.activation(T.d1[:, QC:QC + 1], q, ActivationFunctionType.Relu, bias=BETA, scale=-1.0).then_inc(sem.aq, 1)
    sync()
    V.wait_ge(sem.aq, 1)

    done(V.tensor_scalar(T.d0[:, 0:QC], T.th[:, :], q, 0.5, AluOpType.is_gt, AluOpType.max))
    sync()
    V.wait_ge(sem.aq, 2)
    done(V.tensor_tensor_scan(T.sc[:, :], T.d0[:, :], T.d1[:, :], 1.0, mult, add))
    sync()
    done(V.tensor_tensor_scan(T.pv[:, :], T.sc[:, QC + 1:W], T.cf[:, :], COEF[DEG], mult, add))
    sync()
    done(V.tensor_scalar(T.yb[:, :], T.s[:, BLK * rank:BLK * rank + BLK], T.pv[:, DEG - 1:DEG], T.sc[:, N1 - 1:N1], mult, mult))

    g.sync.wait_ge(sem.vq, n[0])
    g.sync.dma_start(T.y[:, :], T.yb[:, :]).then_inc(sem.st, 16)
    g.sync.wait_ge(sem.st, 16)
